import numpy as np
import ml_dtypes


def mxq(x, axis, fmt="e4m3"):
    dtype, down = {"e4m3": (ml_dtypes.float8_e4m3fn, 7), "e5m2": (ml_dtypes.float8_e5m2, 14)}[fmt]
    v = np.moveaxis(np.asarray(x, np.float32).astype(ml_dtypes.bfloat16).astype(np.float64), axis, -1)
    blocks = v.reshape(v.shape[:-1] + (-1, 32))
    amax = np.abs(blocks).max(-1, keepdims=True)
    byte = np.maximum(np.where(amax > 0, np.frexp(amax)[1] - 1 + 127, 0) - down, 1)
    scale = np.exp2(byte - 127.0)
    codes = (blocks / scale).astype(np.float32).astype(dtype).astype(np.float64)
    return np.moveaxis((codes * scale).reshape(v.shape), -1, axis)


WIDE = False


def mx_kscale(k):
    if not WIDE:
        return np.ones(k)
    levels = np.array([10, -10, 5, -5, 0])
    if k % 512:
        return np.exp2(np.random.permutation(np.resize(levels, k // 32))).repeat(32)
    a = np.empty((k // 512, 16))
    for p in range(k // 512):
        a[p, :8] = np.random.permutation(np.resize(levels, 8))
        for g in range(8):
            far = levels[np.abs(levels - a[p, g]) >= 10]
            a[p, g + 8] = far[np.random.randint(len(far))]
    return np.exp2(a.ravel()).repeat(32)


def f64(x):
    return np.asarray(x).astype(np.float64)


def striped(idx):
    return np.tile(idx.reshape(-1, 16).T, (8, 1)).astype(np.uint16)


def unstriped(offs):
    return offs[:16].T.reshape(-1).astype(np.int64)


E2M1 = np.array([0.0, 0.5, 1.0, 1.5, 2.0, 3.0, 4.0, 6.0, -0.0, -0.5, -1.0, -1.5, -2.0, -3.0, -4.0, -6.0])


def pack_weight(w, fmt):
    k, n = w.shape
    w = f64(np.asarray(w, np.float32).astype(ml_dtypes.bfloat16)).reshape(k // 32, 32, n)
    amax = np.abs(w).max(1)
    if fmt == "e4m3":
        byte = np.frexp(amax)[1] - 1 + 127 - 7
    else:
        mant, ex = np.frexp(amax / 6.0)
        byte = np.where(mant > 0.5, ex, ex - 1) + 127
    byte = np.clip(np.where(amax > 0, byte, 1), 1, 254)
    scaled = (w * np.exp2(127.0 - byte)[:, None, :]).reshape(k, n).astype(np.float32)
    by_word = np.ascontiguousarray(scaled.reshape(k // 512, 128, 4, n).transpose(0, 1, 3, 2))
    if fmt == "e4m3":
        words = by_word.astype(ml_dtypes.float8_e4m3fn).view(np.uint8)
    else:
        c = by_word.astype(ml_dtypes.float4_e2m1fn).view(np.uint8) & 0xF
        words = (c[..., 0::2] | (c[..., 1::2] << 4)).reshape(k // 512, 128, 2 * n)
    return np.ascontiguousarray(words), np.ascontiguousarray(byte.astype(np.uint8).reshape(k // 512, 16, n))


def unpack_weight(words, scales, fmt):
    g, _, n = scales.shape
    words = np.ascontiguousarray(words).reshape(g, 128, n, -1)
    if fmt == "e4m3":
        vals = words.view(ml_dtypes.float8_e4m3fn).astype(np.float64)
    else:
        nib = np.empty((g, 128, n, 4), np.uint8)
        nib[..., 0::2] = words & 0xF
        nib[..., 1::2] = words >> 4
        vals = E2M1[nib]
    vals = vals * np.repeat(np.exp2(scales.astype(np.float64) - 127.0), 8, axis=1)[..., None]
    return vals.transpose(0, 1, 3, 2).reshape(g * 512, n)


def gelu(v):
    return 0.5 * v * (1.0 + np.tanh(np.sqrt(2.0 / np.pi) * (v + 0.044715 * v**3)))


K, T, S, H, T3, S2 = 1536, 2048, 512, 1024, 2048, 512


def setup_inputs():
    n = np.random.standard_normal
    s = mx_kscale(K)[:, None]
    u = mx_kscale(H)[:, None]
    tab_words, tab_scales = pack_weight(n((K, T)) * s, "e4m3")
    tab2_words, tab2_scales = pack_weight(1.2 * n((H, T3)) / np.sqrt(H) / u, "e4m3")
    tab3_words, tab3_scales = pack_weight(n((H, T3)) / np.sqrt(H) / u, "e4m3")
    w1 = (n((K, H)) / np.sqrt(K) / s * u.T).astype(np.float32)
    w4_words, w4_scales = pack_weight(n((K, H)) / np.sqrt(K) / s * u.T, "e2m1")
    return {"tab_words": tab_words, "tab_scales": tab_scales,
            "offs": striped(np.random.permutation(T)[:S]),
            "tab2_words": tab2_words, "tab2_scales": tab2_scales,
            "offs2": striped(np.random.permutation(T3)[:S2]),
            "tab3_words": tab3_words, "tab3_scales": tab3_scales,
            "offs3": striped(np.random.permutation(T3)[:S2]),
            "w1": w1, "w4_words": w4_words, "w4_scales": w4_scales,
            "prior": (0.7 * n((S2, S))).astype(np.float32)}


def reference(tab_words, tab_scales, offs, tab2_words, tab2_scales, offs2,
              tab3_words, tab3_scales, offs3, w1, w4_words, w4_scales, prior):
    v = unpack_weight(tab_words, tab_scales, "e4m3")[:, unstriped(offs)]
    v2 = unpack_weight(tab2_words, tab2_scales, "e4m3")[:, unstriped(offs2)]
    v3 = unpack_weight(tab3_words, tab3_scales, "e4m3")[:, unstriped(offs3)]
    w4 = unpack_weight(w4_words, w4_scales, "e2m1")
    h1 = mxq(f64(w1), 0, "e4m3").T @ v
    h2 = w4.T @ v
    hi = mxq(np.maximum(h1, h2), 0, "e4m3")
    lo = mxq(np.minimum(h1, h2), 0, "e4m3")
    e2 = v2.T @ hi
    e3 = v3.T @ lo
    return np.tanh(e2) * e3 + f64(prior)

@@ -1,0 +1,311 @@
+from contextlib import ExitStack
+
+import concourse.mybir as mybir
+
+K, T, S, H = 1536, 2048, 512, 1024
+FLOPS = 2 * 2 * K * H * S + 2 * 2 * H * S * S
+
+F32 = mybir.dt.float32
+BF16 = mybir.dt.bfloat16
+I32 = mybir.dt.int32
+U32 = mybir.dt.uint32
+U16 = mybir.dt.uint16
+U8 = mybir.dt.uint8
+FP8X4 = mybir.dt.float8_e4m3fn_x4
+FP4X4 = mybir.dt.float4_e2m1fn_x4
+ALU = mybir.AluOpType
+ACT = mybir.ActivationFunctionType
+
+P = 128
+PACK = 4
+PASS = P * PACK
+K_PASSES = K // PASS
+R_BLOCKS = H // PASS
+QUADS = 4
+ROWS = 16
+CHUNK = 128
+CHUNKS = S // CHUNK
+HALF = S // 2
+FIRST_K_ROW = P - ROWS * K_PASSES
+PAIR_ROW = P - 2 * ROWS
+R_PLANE = 4
+
+
+def tile_list_limb_matching_conference_kernel(
+    tc, tab_words, tab_scales, offs, tab2_words, tab2_scales, offs2,
+    tab3_words, tab3_scales, offs3, w1, w4_words, w4_scales, prior, out,
+):
+    nc = tc.nc
+    with ExitStack() as ctx:
+        keep = ctx.enter_context(tc.tile_pool(name="keep", bufs=1))
+        psum = ctx.enter_context(tc.psum_pool(name="psum", bufs=1))
+
+        def held(shape, dtype, name):
+            return keep.tile(shape, dtype, name=name, align_bytes=64)
+
+        def streamed(slot, shape, dtype, name):
+            return keep.tile(shape, dtype, name=name, tag="slot%d" % slot, align_bytes=64)
+
+        list1 = keep.tile([P, S // 16], U16, name="list1")
+        list2 = keep.tile([P, S // 16], U16, name="list2")
+        list3 = keep.tile([P, S // 16], U16, name="list3")
+
+        v_rows = held([P, T], U8, "v_rows")
+        w4_rows = held([P, H], U8, "w4_rows")
+        v2_rows = streamed(1, [P, T], U8, "v2_rows")
+        v3_rows = streamed(2, [P, T], U8, "v3_rows")
+        pair_planes = held([P, 2, S + H], U8, "pair_planes")
+        last_plane = held([P, S + H], U8, "last_plane")
+        k_plane = [pair_planes[:, 0, :], pair_planes[:, 1, :], last_plane[:]]
+        r_planes = held([P, R_BLOCKS, 2 * S], U8, "r_planes")
+        r_rows = ROWS * R_BLOCKS
+
+        nc.vector.memset(v_rows[0:FIRST_K_ROW, :].bitcast(I32), 0)
+        nc.vector.memset(w4_rows[0:FIRST_K_ROW, :].bitcast(I32), 0)
+        for rows in (v2_rows, v3_rows):
+            nc.vector.memset(rows[r_rows : 2 * r_rows, :].bitcast(I32), 0)
+            nc.vector.memset(rows[2 * r_rows : P, :].bitcast(I32), 0)
+        nc.gpsimd.memset(pair_planes[:].rearrange("p a c -> p (a c)").bitcast(I32), 0)
+        nc.gpsimd.memset(last_plane[:].bitcast(I32), 0)
+        nc.gpsimd.memset(r_planes[:].rearrange("p a c -> p (a c)").bitcast(I32), 0)
+
+        def by_row(scales):
+            return scales.bitcast(I32).rearrange("a q t -> q a t")
+
+        def load_words(slot, words, a, name):
+            tile = streamed(slot, [P, T], U32, name)
+            nc.sync.dma_start(out=tile[:].bitcast(I32), in_=words[a].rearrange("p t i -> p (t i)").bitcast(I32))
+            return tile
+
+        def load_w1(slot, b, a):
+            raw = streamed(slot, [P, PACK, PASS], F32, "w1_raw_%d_%d" % (b, a))
+            rows = w1[a * PASS : (a + 1) * PASS, b * PASS : (b + 1) * PASS]
+            nc.sync.dma_start(out=raw[:], in_=rows.rearrange("(p j) c -> p j c", j=PACK))
+            return raw
+
+        nc.sync.dma_start(out=list1[:], in_=offs)
+        for rows, scales in ((v_rows, tab_scales), (w4_rows, w4_scales)):
+            nc.sync.dma_start(out=rows[PAIR_ROW:P, :].bitcast(I32), in_=by_row(scales[0:2]))
+            nc.sync.dma_start(out=rows[FIRST_K_ROW:PAIR_ROW, :].bitcast(I32), in_=scales[2].bitcast(I32))
+        w4_raw = streamed(3, [P, K_PASSES, H], U16, "w4_raw")
+        nc.sync.dma_start(out=w4_raw[:].bitcast(I32), in_=w4_words.bitcast(I32).rearrange("a p c -> p a c"))
+        w1_raw = {(0, 0): load_w1(4, 0, 0)}
+        nc.sync.dma_start(out=list2[:], in_=offs2)
+        nc.sync.dma_start(out=v2_rows[0:r_rows, :].bitcast(I32), in_=by_row(tab2_scales))
+        nc.sync.dma_start(out=list3[:], in_=offs3)
+        nc.sync.dma_start(out=v3_rows[0:r_rows, :].bitcast(I32), in_=by_row(tab3_scales))
+        v_table = [load_words(5, tab_words, 0, "v_table0")]
+
+        v_picked_rows = streamed(0, [P, S], U8, "v_picked_rows")
+        k_rows = held([P, S + H], U8, "k_rows")
+        nc.vector.tensor_copy(out=v_picked_rows[:], in_=v_rows[:].indirect(list1[:]))
+        nc.vector.tensor_copy(
+            out=k_rows[:, S:].rearrange("p (b t g m) -> p b g t m", b=R_BLOCKS, t=PACK, m=16),
+            in_=w4_rows[:].rearrange("p (b g m t) -> p b g t m", b=R_BLOCKS, t=PACK, m=16),
+        )
+        nc.vector.tensor_copy(out=k_rows[:, 0:S].bitcast(I32), in_=v_picked_rows[:].bitcast(I32))
+        for q in range(QUADS):
+            first = PAIR_ROW + 2 * PACK * q
+            nc.sync.dma_start(
+                out=pair_planes[32 * q : 32 * q + PACK, :, :].bitcast(I32),
+                in_=k_rows[first : first + 2 * PACK, :].bitcast(I32),
+            )
+        v_table.append(load_words(0, tab_words, 1, "v_table1"))
+        for q in range(QUADS):
+            first = FIRST_K_ROW + PACK * q
+            nc.sync.dma_start(
+                out=last_plane[32 * q : 32 * q + PACK, :].bitcast(I32),
+                in_=k_rows[first : first + PACK, :].bitcast(I32),
+            )
+        r_picked_rows = held([P, 2 * S], U8, "r_picked_rows")
+        nc.vector.tensor_copy(out=r_picked_rows[:, 0:S], in_=v2_rows[:].indirect(list2[:]))
+        v_table.append(load_words(1, tab_words, 2, "v_table2"))
+        nc.vector.tensor_copy(out=r_picked_rows[:, S:], in_=v3_rows[:].indirect(list3[:]))
+        per_quad = PACK * R_BLOCKS
+        for q in range(QUADS):
+            nc.sync.dma_start(
+                out=r_planes[32 * q + R_PLANE : 32 * q + R_PLANE + PACK, :, :].bitcast(I32),
+                in_=r_picked_rows[per_quad * q : per_quad * (q + 1), :].bitcast(I32),
+            )
+
+        w1_raw[(0, 1)] = load_w1(2, 0, 1)
+
+        w4_codes = held([P, K_PASSES, H], U16, "w4_codes")
+        for a in range(K_PASSES):
+            nc.vector.tensor_copy(
+                out=w4_codes[:, a, :].rearrange("p (b t g m) -> p b g t m", b=R_BLOCKS, t=PACK, m=8),
+                in_=w4_raw[:, a, :].rearrange("p (b g m t) -> p b g t m", b=R_BLOCKS, t=PACK, m=8),
+            )
+
+        w1_raw[(0, 2)] = load_w1(3, 0, 2)
+
+        def gather_words(table, offsets, name, pieces=1):
+            picked = held([P, S], U32, name)
+            n = S // pieces
+            for i in range(pieces):
+                nc.vector.tensor_copy(
+                    out=picked[:, i * n : (i + 1) * n],
+                    in_=table[:].indirect(offsets[:, i * n // 16 : (i + 1) * n // 16]),
+                )
+            return picked
+
+        w1_codes = {}
+        w1_plane = {}
+
+        def quantise_w1(b, a, engine):
+            grouped = keep.tile([P, PACK * PASS], BF16, name="w1_bf16_%d_%d" % (b, a), tag="w1_bf16", bufs=3, align_bytes=64)
+            dst = grouped[:].rearrange("p (t m j) -> p m t j", t=PACK, j=PACK)
+            src = w1_raw[(b, a)][:].rearrange("p j (m t) -> p m t j", t=PACK)
+            if engine == "scalar":
+                nc.scalar.copy(out=dst, in_=src)
+            else:
+                nc.vector.tensor_copy(out=dst, in_=src)
+            codes = held([P, PASS], U32, "w1_codes_%d_%d" % (b, a))
+            plane = held([P, PASS], U8, "w1_plane_%d_%d" % (b, a))
+            nc.vector.quantize_mx(out=codes[:].bitcast(FP8X4), scales=plane[:], in_=grouped[:])
+            w1_codes[(b, a)] = codes
+            w1_plane[(b, a)] = plane
+
+        def banks(group, name):
+            return [psum.tile([P, PASS], F32, name="%s%d" % (name, i), tag="%s%d" % (group, i)) for i in range(4)]
+
+        v_codes = []
+
+        def h2_pass(bank, b, a):
+            for jh in range(2):
+                cols = slice(jh * HALF, (jh + 1) * HALF)
+                for u in range(2):
+                    for e in range(2):
+                        first = b * PASS + (2 * u + e) * P
+                        nc.tensor.matmul_mx(
+                            out=bank[2 * jh + u][:, e * HALF : (e + 1) * HALF],
+                            lhsT=w4_codes[:, a, first : first + P].bitcast(FP4X4),
+                            lhsT_scale=k_plane[a][:, S + first : S + first + P],
+                            rhs=v_codes[a][:, cols].bitcast(FP8X4),
+                            rhs_scale=k_plane[a][:, cols],
+                            start=(a == 0 and e == 0),
+                            stop=(a == K_PASSES - 1 and e == 1),
+                        )
+
+        def h2_out(bank, b):
+            halves = []
+            for jh in range(2):
+                h2 = held([P, 2, HALF, 2], F32, "h2_%d_%d" % (b, jh))
+                for u in range(2):
+                    nc.scalar.copy(out=h2[:, u, :, :], in_=bank[2 * jh + u][:].rearrange("p (e j) -> p j e", e=2))
+                halves.append(h2)
+            return halves
+
+        def h1_pass(bank, b, a):
+            for c in range(CHUNKS):
+                cols = slice(c * CHUNK, (c + 1) * CHUNK)
+                for t in range(PACK):
+                    nc.tensor.matmul_mx(
+                        out=bank[c][:, t * CHUNK : (t + 1) * CHUNK],
+                        lhsT=w1_codes[(b, a)][:, t * P : (t + 1) * P].bitcast(FP8X4),
+                        lhsT_scale=w1_plane[(b, a)][:, t * P : (t + 1) * P],
+                        rhs=v_codes[a][:, cols].bitcast(FP8X4),
+                        rhs_scale=k_plane[a][:, cols],
+                        start=(a == 0 and t == 0),
+                        stop=(a == K_PASSES - 1 and t == PACK - 1),
+                    )
+
+        def extreme(dst, bank, h2, c, op):
+            j0 = (c % 2) * CHUNK
+            nc.vector.tensor_tensor(
+                out=dst[:, c * PASS : (c + 1) * PASS].rearrange("p (j u e) -> p j u e", u=2, e=2),
+                in0=bank[c][:].rearrange("p (u e j) -> p j u e", u=2, e=2),
+                in1=h2[c // 2][:, :, j0 : j0 + CHUNK, :].rearrange("p u j e -> p j u e"),
+                op=op,
+            )
+
+        def quantise_h(src, name):
+            codes = held([P, S], U32, name + "_codes")
+            plane = held([P, S], U8, name + "_plane")
+            nc.vector.quantize_mx(out=codes[:].bitcast(FP8X4), scales=plane[:], in_=src[:])
+            return codes, plane
+
+        def e_pass(bank, picked, first, h, b):
+            for mt in range(4):
+                nc.tensor.matmul_mx(
+                    out=bank[mt][:],
+                    lhsT=picked[:, mt * P : (mt + 1) * P].bitcast(FP8X4),
+                    lhsT_scale=r_planes[R_PLANE:P, b, first + mt * P : first + (mt + 1) * P],
+                    rhs=h[0][:].bitcast(FP8X4),
+                    rhs_scale=h[1][:],
+                    start=(b == 0),
+                    stop=(b == R_BLOCKS - 1),
+                )
+
+        v_codes.append(gather_words(v_table[0], list1, "v_codes0"))
+        w1_raw[(1, 0)] = load_w1(5, 1, 0)
+        quantise_w1(0, 0, "scalar")
+        h2_bank = banks("low", "h2_first")
+        h2_pass(h2_bank, 0, 0)
+        v_codes.append(gather_words(v_table[1], list1, "v_codes1"))
+        w1_raw[(1, 1)] = load_w1(0, 1, 1)
+        w1_raw[(1, 2)] = load_w1(4, 1, 2)
+        h2_pass(h2_bank, 0, 1)
+        h1_bank = banks("high", "h1_first")
+        h1_pass(h1_bank, 0, 0)
+        v_codes.append(gather_words(v_table[2], list1, "v_codes2"))
+        h2_pass(h2_bank, 0, 2)
+        h2_first = h2_out(h2_bank, 0)
+        for a in (1, 2):
+            quantise_w1(0, a, "vector")
+            h1_pass(h1_bank, 0, a)
+        h2_bank = banks("low", "h2_second")
+        for a in range(K_PASSES):
+            h2_pass(h2_bank, 1, a)
+        h2_second = h2_out(h2_bank, 1)
+        quantise_w1(1, 0, "scalar")
+
+        v2_table = [load_words(1 + b, tab2_words, b, "v2_table%d" % b) for b in range(R_BLOCKS)]
+        v3_table = [load_words(3 + 2 * b, tab3_words, b, "v3_table%d" % b) for b in range(R_BLOCKS)]
+
+        hi_first = held([P, PACK * S], BF16, "hi_first")
+        lo_first = held([P, PACK * S], BF16, "lo_first")
+        for c in range(CHUNKS):
+            extreme(hi_first, h1_bank, h2_first, c, ALU.max)
+            extreme(lo_first, h1_bank, h2_first, c, ALU.min)
+        quantise_w1(1, 1, "scalar")
+        sums = streamed(0, [P, 4, S], F32, "sums")
+        for i in range(2):
+            rows = prior[2 * i * P : 2 * (i + 1) * P, :]
+            nc.sync.dma_start(out=sums[:, 2 * i : 2 * i + 2, :], in_=rows.rearrange("(m p) j -> p m j", p=P))
+        result = [sums[:, mt, :] for mt in range(4)]
+        hi = [quantise_h(hi_first, "hi0")]
+        lo = [quantise_h(lo_first, "lo0")]
+        quantise_w1(1, 2, "scalar")
+        h1_bank = banks("high", "h1_second")
+        for a in range(K_PASSES):
+            h1_pass(h1_bank, 1, a)
+
+        e2_bank = banks("low", "e2")
+        e_pass(e2_bank, gather_words(v2_table[0], list2, "v2_codes0"), 0, hi[0], 0)
+        hi_second = held([P, PACK * S], BF16, "hi_second")
+        lo_second = held([P, PACK * S], BF16, "lo_second")
+        for c in range(CHUNKS):
+            extreme(hi_second, h1_bank, h2_second, c, ALU.max)
+        extreme(lo_second, h1_bank, h2_second, 0, ALU.min)
+        hi.append(quantise_h(hi_second, "hi1"))
+        e_pass(e2_bank, gather_words(v2_table[1], list2, "v2_codes1"), 0, hi[1], 1)
+        for c in range(1, CHUNKS):
+            extreme(lo_second, h1_bank, h2_second, c, ALU.min)
+        gate = []
+        for mt in range(4):
+            tile = held([P, S], F32, "gate%d" % mt)
+            nc.scalar.activation(out=tile[:], in_=e2_bank[mt][:], func=ACT.Tanh)
+            gate.append(tile)
+        e3_bank = banks("high", "e3")
+        e_pass(e3_bank, gather_words(v3_table[0], list3, "v3_codes0"), S, lo[0], 0)
+        lo.append(quantise_h(lo_second, "lo1"))
+        e_pass(e3_bank, gather_words(v3_table[1], list3, "v3_codes1", pieces=2), S, lo[1], 1)
+
+        for mt in range(4):
+            nc.vector.tensor_tensor(out=gate[mt][:], in0=e3_bank[mt][:], in1=gate[mt][:], op=ALU.mult)
+            if mt > 0:
+                nc.vector.tensor_tensor(out=result[mt - 1], in0=result[mt - 1], in1=gate[mt - 1][:], op=ALU.add)
+                nc.sync.dma_start(out=out[(mt - 1) * P : mt * P, :], in_=result[mt - 1])
+        nc.vector.tensor_tensor(out=result[3], in0=result[3], in1=gate[3][:], op=ALU.add)
+        nc.sync.dma_start(out=out[3 * P : 4 * P, :], in_=result[3])

@@ -21,11 +21,10 @@ PACK = 4
 PASS = P * PACK
 K_PASSES = K // PASS
 R_BLOCKS = H // PASS
-QUADS = 4
 ROWS = 16
 CHUNK = 128
 CHUNKS = S // CHUNK
-HALF = S // 2
+QUAD_ORDER = (0, 2, 1, 3)
 FIRST_K_ROW = P - ROWS * K_PASSES
 PAIR_ROW = P - 2 * ROWS
 R_PLANE = 4
@@ -52,8 +51,8 @@ def tile_list_limb_matching_conference_kernel(
 
         v_rows = held([P, T], U8, "v_rows")
         w4_rows = held([P, H], U8, "w4_rows")
-        v2_rows = streamed(1, [P, T], U8, "v2_rows")
-        v3_rows = streamed(2, [P, T], U8, "v3_rows")
+        v2_rows = streamed(3, [P, T], U8, "v2_rows")
+        v3_rows = streamed(4, [P, T], U8, "v3_rows")
         pair_planes = held([P, 2, S + H], U8, "pair_planes")
         last_plane = held([P, S + H], U8, "last_plane")
         k_plane = [pair_planes[:, 0, :], pair_planes[:, 1, :], last_plane[:]]
@@ -87,14 +86,13 @@ def tile_list_limb_matching_conference_kernel(
         for rows, scales in ((v_rows, tab_scales), (w4_rows, w4_scales)):
             nc.sync.dma_start(out=rows[PAIR_ROW:P, :].bitcast(I32), in_=by_row(scales[0:2]))
             nc.sync.dma_start(out=rows[FIRST_K_ROW:PAIR_ROW, :].bitcast(I32), in_=scales[2].bitcast(I32))
-        w4_raw = streamed(3, [P, K_PASSES, H], U16, "w4_raw")
+        w4_raw = streamed(1, [P, K_PASSES, H], U16, "w4_raw")
         nc.sync.dma_start(out=w4_raw[:].bitcast(I32), in_=w4_words.bitcast(I32).rearrange("a p c -> p a c"))
-        w1_raw = {(0, 0): load_w1(4, 0, 0)}
         nc.sync.dma_start(out=list2[:], in_=offs2)
         nc.sync.dma_start(out=v2_rows[0:r_rows, :].bitcast(I32), in_=by_row(tab2_scales))
         nc.sync.dma_start(out=list3[:], in_=offs3)
         nc.sync.dma_start(out=v3_rows[0:r_rows, :].bitcast(I32), in_=by_row(tab3_scales))
-        v_table = [load_words(5, tab_words, 0, "v_table0")]
+        v_table = [load_words(2, tab_words, 0, "v_table0")]
 
         v_picked_rows = streamed(0, [P, S], U8, "v_picked_rows")
         k_rows = held([P, S + H], U8, "k_rows")
@@ -104,32 +102,19 @@ def tile_list_limb_matching_conference_kernel(
             in_=w4_rows[:].rearrange("p (b g m t) -> p b g t m", b=R_BLOCKS, t=PACK, m=16),
         )
         nc.vector.tensor_copy(out=k_rows[:, 0:S].bitcast(I32), in_=v_picked_rows[:].bitcast(I32))
-        for q in range(QUADS):
+        for q in QUAD_ORDER:
             first = PAIR_ROW + 2 * PACK * q
             nc.sync.dma_start(
                 out=pair_planes[32 * q : 32 * q + PACK, :, :].bitcast(I32),
                 in_=k_rows[first : first + 2 * PACK, :].bitcast(I32),
             )
         v_table.append(load_words(0, tab_words, 1, "v_table1"))
-        for q in range(QUADS):
+        for q in QUAD_ORDER:
             first = FIRST_K_ROW + PACK * q
             nc.sync.dma_start(
                 out=last_plane[32 * q : 32 * q + PACK, :].bitcast(I32),
                 in_=k_rows[first : first + PACK, :].bitcast(I32),
             )
-        r_picked_rows = held([P, 2 * S], U8, "r_picked_rows")
-        nc.vector.tensor_copy(out=r_picked_rows[:, 0:S], in_=v2_rows[:].indirect(list2[:]))
-        v_table.append(load_words(1, tab_words, 2, "v_table2"))
-        nc.vector.tensor_copy(out=r_picked_rows[:, S:], in_=v3_rows[:].indirect(list3[:]))
-        per_quad = PACK * R_BLOCKS
-        for q in range(QUADS):
-            nc.sync.dma_start(
-                out=r_planes[32 * q + R_PLANE : 32 * q + R_PLANE + PACK, :, :].bitcast(I32),
-                in_=r_picked_rows[per_quad * q : per_quad * (q + 1), :].bitcast(I32),
-            )
-
-        w1_raw[(0, 1)] = load_w1(2, 0, 1)
-
         w4_codes = held([P, K_PASSES, H], U16, "w4_codes")
         for a in range(K_PASSES):
             nc.vector.tensor_copy(
@@ -137,7 +122,7 @@ def tile_list_limb_matching_conference_kernel(
                 in_=w4_raw[:, a, :].rearrange("p (b g m t) -> p b g t m", b=R_BLOCKS, t=PACK, m=8),
             )
 
-        w1_raw[(0, 2)] = load_w1(3, 0, 2)
+        w1_raw = {(0, 0): load_w1(1, 0, 0)}
 
         def gather_words(table, offsets, name, pieces=1):
             picked = held([P, S], U32, name)
@@ -152,8 +137,10 @@ def tile_list_limb_matching_conference_kernel(
         w1_codes = {}
         w1_plane = {}
 
-        def quantise_w1(b, a, engine):
-            grouped = keep.tile([P, PACK * PASS], BF16, name="w1_bf16_%d_%d" % (b, a), tag="w1_bf16", bufs=3, align_bytes=64)
+        def quantise_w1(b, a, engine, slot=None):
+            name = "w1_bf16_%d_%d" % (b, a)
+            shape = [P, PACK * PASS]
+            grouped = held(shape, BF16, name) if slot is None else streamed(slot, shape, BF16, name)
             dst = grouped[:].rearrange("p (t m j) -> p m t j", t=PACK, j=PACK)
             src = w1_raw[(b, a)][:].rearrange("p j (m t) -> p m t j", t=PACK)
             if engine == "scalar":
@@ -172,29 +159,27 @@ def tile_list_limb_matching_conference_kernel(
         v_codes = []
 
         def h2_pass(bank, b, a):
-            for jh in range(2):
-                cols = slice(jh * HALF, (jh + 1) * HALF)
-                for u in range(2):
-                    for e in range(2):
-                        first = b * PASS + (2 * u + e) * P
-                        nc.tensor.matmul_mx(
-                            out=bank[2 * jh + u][:, e * HALF : (e + 1) * HALF],
-                            lhsT=w4_codes[:, a, first : first + P].bitcast(FP4X4),
-                            lhsT_scale=k_plane[a][:, S + first : S + first + P],
-                            rhs=v_codes[a][:, cols].bitcast(FP8X4),
-                            rhs_scale=k_plane[a][:, cols],
-                            start=(a == 0 and e == 0),
-                            stop=(a == K_PASSES - 1 and e == 1),
-                        )
+            for c in range(CHUNKS):
+                cols = slice(c * CHUNK, (c + 1) * CHUNK)
+                for t in range(PACK):
+                    first = b * PASS + t * P
+                    nc.tensor.matmul_mx(
+                        out=bank[c][:, t * CHUNK : (t + 1) * CHUNK],
+                        lhsT=w4_codes[:, a, first : first + P].bitcast(FP4X4),
+                        lhsT_scale=k_plane[a][:, S + first : S + first + P],
+                        rhs=v_codes[a][:, cols].bitcast(FP8X4),
+                        rhs_scale=k_plane[a][:, cols],
+                        start=(a == 0 and t == 0),
+                        stop=(a == K_PASSES - 1 and t == PACK - 1),
+                    )
 
         def h2_out(bank, b):
-            halves = []
-            for jh in range(2):
-                h2 = held([P, 2, HALF, 2], F32, "h2_%d_%d" % (b, jh))
-                for u in range(2):
-                    nc.scalar.copy(out=h2[:, u, :, :], in_=bank[2 * jh + u][:].rearrange("p (e j) -> p j e", e=2))
-                halves.append(h2)
-            return halves
+            chunks = []
+            for c in range(CHUNKS):
+                h2 = held([P, CHUNK, PACK], F32, "h2_%d_%d" % (b, c))
+                nc.scalar.copy(out=h2[:], in_=bank[c][:].rearrange("p (t j) -> p j t", t=PACK))
+                chunks.append(h2)
+            return chunks
 
         def h1_pass(bank, b, a):
             for c in range(CHUNKS):
@@ -211,11 +196,10 @@ def tile_list_limb_matching_conference_kernel(
                     )
 
         def extreme(dst, bank, h2, c, op):
-            j0 = (c % 2) * CHUNK
             nc.vector.tensor_tensor(
-                out=dst[:, c * PASS : (c + 1) * PASS].rearrange("p (j u e) -> p j u e", u=2, e=2),
-                in0=bank[c][:].rearrange("p (u e j) -> p j u e", u=2, e=2),
-                in1=h2[c // 2][:, :, j0 : j0 + CHUNK, :].rearrange("p u j e -> p j u e"),
+                out=dst[:, c * PASS : (c + 1) * PASS].rearrange("p (j t) -> p j t", t=PACK),
+                in0=bank[c][:].rearrange("p (t j) -> p j t", t=PACK),
+                in1=h2[c][:],
                 op=op,
             )
 
@@ -237,31 +221,43 @@ def tile_list_limb_matching_conference_kernel(
                     stop=(b == R_BLOCKS - 1),
                 )
 
+        h2_bank = [banks("low", "h2_first"), banks("high", "h2_second")]
         v_codes.append(gather_words(v_table[0], list1, "v_codes0"))
-        w1_raw[(1, 0)] = load_w1(5, 1, 0)
-        quantise_w1(0, 0, "scalar")
-        h2_bank = banks("low", "h2_first")
-        h2_pass(h2_bank, 0, 0)
+        for b in range(R_BLOCKS):
+            h2_pass(h2_bank[b], b, 0)
+        r_picked_rows = streamed(2, [P, 2 * S], U8, "r_picked_rows")
+        nc.vector.tensor_copy(out=r_picked_rows[:, 0:S], in_=v2_rows[:].indirect(list2[:]))
+        v_table.append(load_words(3, tab_words, 2, "v_table2"))
         v_codes.append(gather_words(v_table[1], list1, "v_codes1"))
-        w1_raw[(1, 1)] = load_w1(0, 1, 1)
-        w1_raw[(1, 2)] = load_w1(4, 1, 2)
-        h2_pass(h2_bank, 0, 1)
-        h1_bank = banks("high", "h1_first")
-        h1_pass(h1_bank, 0, 0)
+        w1_raw[(0, 1)] = load_w1(0, 0, 1)
+        for b in range(R_BLOCKS):
+            h2_pass(h2_bank[b], b, 1)
+        nc.vector.tensor_copy(out=r_picked_rows[:, S:], in_=v3_rows[:].indirect(list3[:]))
+        w1_raw[(0, 2)] = load_w1(4, 0, 2)
+        per_quad = PACK * R_BLOCKS
+        for q in QUAD_ORDER:
+            nc.gpsimd.dma_start(
+                out=r_planes[32 * q + R_PLANE : 32 * q + R_PLANE + PACK, :, :].bitcast(I32),
+                in_=r_picked_rows[per_quad * q : per_quad * (q + 1), :].bitcast(I32),
+            )
         v_codes.append(gather_words(v_table[2], list1, "v_codes2"))
-        h2_pass(h2_bank, 0, 2)
-        h2_first = h2_out(h2_bank, 0)
-        for a in (1, 2):
-            quantise_w1(0, a, "vector")
-            h1_pass(h1_bank, 0, a)
-        h2_bank = banks("low", "h2_second")
-        for a in range(K_PASSES):
-            h2_pass(h2_bank, 1, a)
-        h2_second = h2_out(h2_bank, 1)
+        quantise_w1(0, 0, "scalar")
+        w1_raw[(1, 0)] = load_w1(1, 1, 0)
+        w1_raw[(1, 1)] = load_w1(3, 1, 1)
+        for b in range(R_BLOCKS):
+            h2_pass(h2_bank[b], b, 2)
+        h2_first = h2_out(h2_bank[0], 0)
+        h2_second = h2_out(h2_bank[1], 1)
+        h1_bank = banks("low", "h1_first")
+        h1_pass(h1_bank, 0, 0)
+        quantise_w1(0, 1, "vector")
+        w1_raw[(1, 2)] = load_w1(0, 1, 2)
+        h1_pass(h1_bank, 0, 1)
+        quantise_w1(0, 2, "vector", slot=5)
+        v2_table = [load_words(4, tab2_words, 0, "v2_table0"), load_words(5, tab2_words, 1, "v2_table1")]
+        h1_pass(h1_bank, 0, 2)
         quantise_w1(1, 0, "scalar")
-
-        v2_table = [load_words(1 + b, tab2_words, b, "v2_table%d" % b) for b in range(R_BLOCKS)]
-        v3_table = [load_words(3 + 2 * b, tab3_words, b, "v3_table%d" % b) for b in range(R_BLOCKS)]
+        v3_table = [load_words(1, tab3_words, 0, "v3_table0")]
 
         hi_first = held([P, PACK * S], BF16, "hi_first")
         lo_first = held([P, PACK * S], BF16, "lo_first")
@@ -269,14 +265,15 @@ def tile_list_limb_matching_conference_kernel(
             extreme(hi_first, h1_bank, h2_first, c, ALU.max)
             extreme(lo_first, h1_bank, h2_first, c, ALU.min)
         quantise_w1(1, 1, "scalar")
+        v3_table.append(load_words(3, tab3_words, 1, "v3_table1"))
+        hi = [quantise_h(hi_first, "hi0")]
+        lo = [quantise_h(lo_first, "lo0")]
+        quantise_w1(1, 2, "scalar")
         sums = streamed(0, [P, 4, S], F32, "sums")
         for i in range(2):
             rows = prior[2 * i * P : 2 * (i + 1) * P, :]
             nc.sync.dma_start(out=sums[:, 2 * i : 2 * i + 2, :], in_=rows.rearrange("(m p) j -> p m j", p=P))
         result = [sums[:, mt, :] for mt in range(4)]
-        hi = [quantise_h(hi_first, "hi0")]
-        lo = [quantise_h(lo_first, "lo0")]
-        quantise_w1(1, 2, "scalar")
         h1_bank = banks("high", "h1_second")
         for a in range(K_PASSES):
             h1_pass(h1_bank, 1, a)
@@ -305,7 +302,8 @@ def tile_list_limb_matching_conference_kernel(
         for mt in range(4):
             nc.vector.tensor_tensor(out=gate[mt][:], in0=e3_bank[mt][:], in1=gate[mt][:], op=ALU.mult)
             if mt > 0:
-                nc.vector.tensor_tensor(out=result[mt - 1], in0=result[mt - 1], in1=gate[mt - 1][:], op=ALU.add)
+                adder = nc.gpsimd if mt == 1 else nc.vector
+                adder.tensor_tensor(out=result[mt - 1], in0=result[mt - 1], in1=gate[mt - 1][:], op=ALU.add)
                 nc.sync.dma_start(out=out[(mt - 1) * P : mt * P, :], in_=result[mt - 1])
         nc.vector.tensor_tensor(out=result[3], in0=result[3], in1=gate[3][:], op=ALU.add)
         nc.sync.dma_start(out=out[3 * P : 4 * P, :], in_=result[3])

@@ -24,6 +24,7 @@ R_BLOCKS = H // PASS
 ROWS = 16
 CHUNK = 128
 CHUNKS = S // CHUNK
+HALF = S // 2
 QUAD_ORDER = (0, 2, 1, 3)
 FIRST_K_ROW = P - ROWS * K_PASSES
 PAIR_ROW = P - 2 * ROWS
@@ -141,15 +142,21 @@ def tile_list_limb_matching_conference_kernel(
             name = "w1_bf16_%d_%d" % (b, a)
             shape = [P, PACK * PASS]
             grouped = held(shape, BF16, name) if slot is None else streamed(slot, shape, BF16, name)
-            dst = grouped[:].rearrange("p (t m j) -> p m t j", t=PACK, j=PACK)
-            src = w1_raw[(b, a)][:].rearrange("p j (m t) -> p m t j", t=PACK)
-            if engine == "scalar":
-                nc.scalar.copy(out=dst, in_=src)
-            else:
-                nc.vector.tensor_copy(out=dst, in_=src)
             codes = held([P, PASS], U32, "w1_codes_%d_%d" % (b, a))
             plane = held([P, PASS], U8, "w1_plane_%d_%d" % (b, a))
-            nc.vector.quantize_mx(out=codes[:].bitcast(FP8X4), scales=plane[:], in_=grouped[:])
+            copy = nc.scalar.copy if engine == "scalar" else nc.vector.tensor_copy
+            for u in range(2):
+                copy(
+                    out=grouped[:, u * 2 * PASS : (u + 1) * 2 * PASS].rearrange("p (e m j) -> p m j e", e=2, j=PACK),
+                    in_=w1_raw[(b, a)][:].rearrange("p j (m u e) -> p u m j e", u=2, e=2)[:, u],
+                )
+            for u in range(2):
+                cols = slice(u * 2 * P, (u + 1) * 2 * P)
+                nc.vector.quantize_mx(
+                    out=codes[:, cols].bitcast(FP8X4),
+                    scales=plane[:, cols],
+                    in_=grouped[:, u * 2 * PASS : (u + 1) * 2 * PASS],
+                )
             w1_codes[(b, a)] = codes
             w1_plane[(b, a)] = plane
 
@@ -159,27 +166,29 @@ def tile_list_limb_matching_conference_kernel(
         v_codes = []
 
         def h2_pass(bank, b, a):
-            for c in range(CHUNKS):
-                cols = slice(c * CHUNK, (c + 1) * CHUNK)
-                for t in range(PACK):
-                    first = b * PASS + t * P
-                    nc.tensor.matmul_mx(
-                        out=bank[c][:, t * CHUNK : (t + 1) * CHUNK],
-                        lhsT=w4_codes[:, a, first : first + P].bitcast(FP4X4),
-                        lhsT_scale=k_plane[a][:, S + first : S + first + P],
-                        rhs=v_codes[a][:, cols].bitcast(FP8X4),
-                        rhs_scale=k_plane[a][:, cols],
-                        start=(a == 0 and t == 0),
-                        stop=(a == K_PASSES - 1 and t == PACK - 1),
-                    )
+            for jh in range(2):
+                cols = slice(jh * HALF, (jh + 1) * HALF)
+                for u in range(2):
+                    for e in range(2):
+                        first = b * PASS + (2 * u + e) * P
+                        nc.tensor.matmul_mx(
+                            out=bank[2 * jh + u][:, e * HALF : (e + 1) * HALF],
+                            lhsT=w4_codes[:, a, first : first + P].bitcast(FP4X4),
+                            lhsT_scale=k_plane[a][:, S + first : S + first + P],
+                            rhs=v_codes[a][:, cols].bitcast(FP8X4),
+                            rhs_scale=k_plane[a][:, cols],
+                            start=(a == 0 and e == 0),
+                            stop=(a == K_PASSES - 1 and e == 1),
+                        )
 
         def h2_out(bank, b):
-            chunks = []
-            for c in range(CHUNKS):
-                h2 = held([P, CHUNK, PACK], F32, "h2_%d_%d" % (b, c))
-                nc.scalar.copy(out=h2[:], in_=bank[c][:].rearrange("p (t j) -> p j t", t=PACK))
-                chunks.append(h2)
-            return chunks
+            halves = []
+            for jh in range(2):
+                h2 = held([P, 2, HALF, 2], F32, "h2_%d_%d" % (b, jh))
+                for u in range(2):
+                    nc.scalar.copy(out=h2[:, u, :, :], in_=bank[2 * jh + u][:].rearrange("p (e j) -> p j e", e=2))
+                halves.append(h2)
+            return halves
 
         def h1_pass(bank, b, a):
             for c in range(CHUNKS):
@@ -196,10 +205,11 @@ def tile_list_limb_matching_conference_kernel(
                     )
 
         def extreme(dst, bank, h2, c, op):
+            j0 = (c % 2) * CHUNK
             nc.vector.tensor_tensor(
-                out=dst[:, c * PASS : (c + 1) * PASS].rearrange("p (j t) -> p j t", t=PACK),
-                in0=bank[c][:].rearrange("p (t j) -> p j t", t=PACK),
-                in1=h2[c][:],
+                out=dst[:, c * PASS : (c + 1) * PASS].rearrange("p (j u e) -> p j u e", u=2, e=2),
+                in0=bank[c][:].rearrange("p (u e j) -> p j u e", u=2, e=2),
+                in1=h2[c // 2][:, :, j0 : j0 + CHUNK, :].rearrange("p u j e -> p j u e"),
                 op=op,
             )
 

@@ -62,10 +62,10 @@ def tile_list_limb_matching_conference_kernel(
 
         nc.vector.memset(v_rows[0:FIRST_K_ROW, :].bitcast(I32), 0)
         nc.vector.memset(w4_rows[0:FIRST_K_ROW, :].bitcast(I32), 0)
+        nc.vector.memset(pair_planes[:].rearrange("p a c -> p (a c)").bitcast(I32), 0)
         for rows in (v2_rows, v3_rows):
             nc.vector.memset(rows[r_rows : 2 * r_rows, :].bitcast(I32), 0)
             nc.vector.memset(rows[2 * r_rows : P, :].bitcast(I32), 0)
-        nc.gpsimd.memset(pair_planes[:].rearrange("p a c -> p (a c)").bitcast(I32), 0)
         nc.gpsimd.memset(last_plane[:].bitcast(I32), 0)
         nc.gpsimd.memset(r_planes[:].rearrange("p a c -> p (a c)").bitcast(I32), 0)
 
@@ -138,18 +138,21 @@ def tile_list_limb_matching_conference_kernel(
         w1_codes = {}
         w1_plane = {}
 
-        def quantise_w1(b, a, engine, slot=None):
+        def round_w1(b, a, copy, slot=None):
             name = "w1_bf16_%d_%d" % (b, a)
             shape = [P, PACK * PASS]
             grouped = held(shape, BF16, name) if slot is None else streamed(slot, shape, BF16, name)
-            codes = held([P, PASS], U32, "w1_codes_%d_%d" % (b, a))
-            plane = held([P, PASS], U8, "w1_plane_%d_%d" % (b, a))
-            copy = nc.scalar.copy if engine == "scalar" else nc.vector.tensor_copy
             for u in range(2):
                 copy(
                     out=grouped[:, u * 2 * PASS : (u + 1) * 2 * PASS].rearrange("p (e m j) -> p m j e", e=2, j=PACK),
                     in_=w1_raw[(b, a)][:].rearrange("p j (m u e) -> p u m j e", u=2, e=2)[:, u],
                 )
+            return grouped
+
+        def quantise_w1(b, a, grouped, slot=None):
+            name = "w1_codes_%d_%d" % (b, a)
+            codes = held([P, PASS], U32, name) if slot is None else streamed(slot, [P, PASS], U32, name)
+            plane = held([P, PASS], U8, "w1_plane_%d_%d" % (b, a))
             for u in range(2):
                 cols = slice(u * 2 * P, (u + 1) * 2 * P)
                 nc.vector.quantize_mx(
@@ -181,10 +184,10 @@ def tile_list_limb_matching_conference_kernel(
                             stop=(a == K_PASSES - 1 and e == 1),
                         )
 
-        def h2_out(bank, b):
+        def h2_out(bank, b, slot):
             halves = []
             for jh in range(2):
-                h2 = held([P, 2, HALF, 2], F32, "h2_%d_%d" % (b, jh))
+                h2 = streamed(slot + jh, [P, 2, HALF, 2], F32, "h2_%d_%d" % (b, jh))
                 for u in range(2):
                     nc.scalar.copy(out=h2[:, u, :, :], in_=bank[2 * jh + u][:].rearrange("p (e j) -> p j e", e=2))
                 halves.append(h2)
@@ -251,22 +254,22 @@ def tile_list_limb_matching_conference_kernel(
                 in_=r_picked_rows[per_quad * q : per_quad * (q + 1), :].bitcast(I32),
             )
         v_codes.append(gather_words(v_table[2], list1, "v_codes2"))
-        quantise_w1(0, 0, "scalar")
+        quantise_w1(0, 0, round_w1(0, 0, nc.scalar.copy))
         w1_raw[(1, 0)] = load_w1(1, 1, 0)
         w1_raw[(1, 1)] = load_w1(3, 1, 1)
         for b in range(R_BLOCKS):
             h2_pass(h2_bank[b], b, 2)
-        h2_first = h2_out(h2_bank[0], 0)
-        h2_second = h2_out(h2_bank[1], 1)
+        h2_first = h2_out(h2_bank[0], 0, 6)
+        h2_second = h2_out(h2_bank[1], 1, 8)
         h1_bank = banks("low", "h1_first")
         h1_pass(h1_bank, 0, 0)
-        quantise_w1(0, 1, "vector")
+        quantise_w1(0, 1, round_w1(0, 1, nc.vector.tensor_copy))
         w1_raw[(1, 2)] = load_w1(0, 1, 2)
         h1_pass(h1_bank, 0, 1)
-        quantise_w1(0, 2, "vector", slot=5)
+        quantise_w1(0, 2, round_w1(0, 2, nc.vector.tensor_copy, slot=5))
         v2_table = [load_words(4, tab2_words, 0, "v2_table0"), load_words(5, tab2_words, 1, "v2_table1")]
         h1_pass(h1_bank, 0, 2)
-        quantise_w1(1, 0, "scalar")
+        rounded = [round_w1(1, 0, nc.scalar.copy)]
         v3_table = [load_words(1, tab3_words, 0, "v3_table0")]
 
         hi_first = held([P, PACK * S], BF16, "hi_first")
@@ -274,22 +277,27 @@ def tile_list_limb_matching_conference_kernel(
         for c in range(CHUNKS):
             extreme(hi_first, h1_bank, h2_first, c, ALU.max)
             extreme(lo_first, h1_bank, h2_first, c, ALU.min)
-        quantise_w1(1, 1, "scalar")
+        rounded.append(round_w1(1, 1, nc.scalar.copy))
         v3_table.append(load_words(3, tab3_words, 1, "v3_table1"))
+        quantise_w1(1, 0, rounded[0], slot=6)
+        quantise_w1(1, 1, rounded[1], slot=7)
         hi = [quantise_h(hi_first, "hi0")]
         lo = [quantise_h(lo_first, "lo0")]
-        quantise_w1(1, 2, "scalar")
+        rounded.append(round_w1(1, 2, nc.scalar.copy))
         sums = streamed(0, [P, 4, S], F32, "sums")
         for i in range(2):
             rows = prior[2 * i * P : 2 * (i + 1) * P, :]
             nc.sync.dma_start(out=sums[:, 2 * i : 2 * i + 2, :], in_=rows.rearrange("(m p) j -> p m j", p=P))
         result = [sums[:, mt, :] for mt in range(4)]
         h1_bank = banks("high", "h1_second")
-        for a in range(K_PASSES):
+        for a in range(K_PASSES - 1):
             h1_pass(h1_bank, 1, a)
+        v2_first = gather_words(v2_table[0], list2, "v2_codes0")
+        quantise_w1(1, 2, rounded[2])
+        h1_pass(h1_bank, 1, 2)
 
         e2_bank = banks("low", "e2")
-        e_pass(e2_bank, gather_words(v2_table[0], list2, "v2_codes0"), 0, hi[0], 0)
+        e_pass(e2_bank, v2_first, 0, hi[0], 0)
         hi_second = held([P, PACK * S], BF16, "hi_second")
         lo_second = held([P, PACK * S], BF16, "lo_second")
         for c in range(CHUNKS):

from contextlib import ExitStack

import concourse.mybir as mybir

K, T, S, H = 1536, 2048, 512, 1024
FLOPS = 2 * 2 * K * H * S + 2 * 2 * H * S * S

F32 = mybir.dt.float32
BF16 = mybir.dt.bfloat16
I32 = mybir.dt.int32
U32 = mybir.dt.uint32
U16 = mybir.dt.uint16
U8 = mybir.dt.uint8
FP8X4 = mybir.dt.float8_e4m3fn_x4
FP4X4 = mybir.dt.float4_e2m1fn_x4
ALU = mybir.AluOpType
ACT = mybir.ActivationFunctionType

P = 128
PACK = 4
PASS = P * PACK
K_PASSES = K // PASS
R_BLOCKS = H // PASS
ROWS = 16
CHUNK = 128
CHUNKS = S // CHUNK
HALF = S // 2
QUAD_ORDER = (0, 2, 1, 3)
FIRST_K_ROW = P - ROWS * K_PASSES
PAIR_ROW = P - 2 * ROWS
R_PLANE = 4


def tile_list_limb_matching_conference_kernel(
    tc, tab_words, tab_scales, offs, tab2_words, tab2_scales, offs2,
    tab3_words, tab3_scales, offs3, w1, w4_words, w4_scales, prior, out,
):
    nc = tc.nc
    with ExitStack() as ctx:
        keep = ctx.enter_context(tc.tile_pool(name="keep", bufs=1))
        psum = ctx.enter_context(tc.psum_pool(name="psum", bufs=1))

        def held(shape, dtype, name):
            return keep.tile(shape, dtype, name=name, align_bytes=64)

        def streamed(slot, shape, dtype, name):
            return keep.tile(shape, dtype, name=name, tag="slot%d" % slot, align_bytes=64)

        list1 = keep.tile([P, S // 16], U16, name="list1")
        list2 = keep.tile([P, S // 16], U16, name="list2")
        list3 = keep.tile([P, S // 16], U16, name="list3")

        v_rows = held([P, T], U8, "v_rows")
        w4_rows = held([P, H], U8, "w4_rows")
        v2_rows = streamed(3, [P, T], U8, "v2_rows")
        v3_rows = streamed(4, [P, T], U8, "v3_rows")
        pair_planes = held([P, 2, S + H], U8, "pair_planes")
        last_plane = held([P, S + H], U8, "last_plane")
        k_plane = [pair_planes[:, 0, :], pair_planes[:, 1, :], last_plane[:]]
        r_planes = held([P, R_BLOCKS, 2 * S], U8, "r_planes")
        r_rows = ROWS * R_BLOCKS

        nc.vector.memset(v_rows[0:FIRST_K_ROW, :].bitcast(I32), 0)
        nc.vector.memset(w4_rows[0:FIRST_K_ROW, :].bitcast(I32), 0)
        nc.vector.memset(pair_planes[:].rearrange("p a c -> p (a c)").bitcast(I32), 0)
        for rows in (v2_rows, v3_rows):
            nc.vector.memset(rows[r_rows : 2 * r_rows, :].bitcast(I32), 0)
            nc.vector.memset(rows[2 * r_rows : P, :].bitcast(I32), 0)
        nc.gpsimd.memset(last_plane[:].bitcast(I32), 0)
        nc.gpsimd.memset(r_planes[:].rearrange("p a c -> p (a c)").bitcast(I32), 0)

        def by_row(scales):
            return scales.bitcast(I32).rearrange("a q t -> q a t")

        def load_words(slot, words, a, name):
            tile = streamed(slot, [P, T], U32, name)
            nc.sync.dma_start(out=tile[:].bitcast(I32), in_=words[a].rearrange("p t i -> p (t i)").bitcast(I32))
            return tile

        def load_w1(slot, b, a):
            raw = streamed(slot, [P, PACK, PASS], F32, "w1_raw_%d_%d" % (b, a))
            rows = w1[a * PASS : (a + 1) * PASS, b * PASS : (b + 1) * PASS]
            nc.sync.dma_start(out=raw[:], in_=rows.rearrange("(p j) c -> p j c", j=PACK))
            return raw

        nc.sync.dma_start(out=list1[:], in_=offs)
        for rows, scales in ((v_rows, tab_scales), (w4_rows, w4_scales)):
            nc.sync.dma_start(out=rows[PAIR_ROW:P, :].bitcast(I32), in_=by_row(scales[0:2]))
            nc.sync.dma_start(out=rows[FIRST_K_ROW:PAIR_ROW, :].bitcast(I32), in_=scales[2].bitcast(I32))
        w4_raw = streamed(1, [P, K_PASSES, H], U16, "w4_raw")
        nc.sync.dma_start(out=w4_raw[:].bitcast(I32), in_=w4_words.bitcast(I32).rearrange("a p c -> p a c"))
        nc.sync.dma_start(out=list2[:], in_=offs2)
        nc.sync.dma_start(out=v2_rows[0:r_rows, :].bitcast(I32), in_=by_row(tab2_scales))
        nc.sync.dma_start(out=list3[:], in_=offs3)
        nc.sync.dma_start(out=v3_rows[0:r_rows, :].bitcast(I32), in_=by_row(tab3_scales))
        v_table = [load_words(2, tab_words, 0, "v_table0")]

        v_picked_rows = streamed(0, [P, S], U8, "v_picked_rows")
        k_rows = held([P, S + H], U8, "k_rows")
        nc.vector.tensor_copy(out=v_picked_rows[:], in_=v_rows[:].indirect(list1[:]))
        nc.vector.tensor_copy(
            out=k_rows[:, S:].rearrange("p (b t g m) -> p b g t m", b=R_BLOCKS, t=PACK, m=16),
            in_=w4_rows[:].rearrange("p (b g m t) -> p b g t m", b=R_BLOCKS, t=PACK, m=16),
        )
        nc.vector.tensor_copy(out=k_rows[:, 0:S].bitcast(I32), in_=v_picked_rows[:].bitcast(I32))
        for q in QUAD_ORDER:
            first = PAIR_ROW + 2 * PACK * q
            nc.sync.dma_start(
                out=pair_planes[32 * q : 32 * q + PACK, :, :].bitcast(I32),
                in_=k_rows[first : first + 2 * PACK, :].bitcast(I32),
            )
        v_table.append(load_words(0, tab_words, 1, "v_table1"))
        for q in QUAD_ORDER:
            first = FIRST_K_ROW + PACK * q
            nc.sync.dma_start(
                out=last_plane[32 * q : 32 * q + PACK, :].bitcast(I32),
                in_=k_rows[first : first + PACK, :].bitcast(I32),
            )
        w4_codes = held([P, K_PASSES, H], U16, "w4_codes")
        for a in range(K_PASSES):
            nc.vector.tensor_copy(
                out=w4_codes[:, a, :].rearrange("p (b t g m) -> p b g t m", b=R_BLOCKS, t=PACK, m=8),
                in_=w4_raw[:, a, :].rearrange("p (b g m t) -> p b g t m", b=R_BLOCKS, t=PACK, m=8),
            )

        w1_raw = {(0, 0): load_w1(1, 0, 0)}

        def gather_words(table, offsets, name, pieces=1):
            picked = held([P, S], U32, name)
            n = S // pieces
            for i in range(pieces):
                nc.vector.tensor_copy(
                    out=picked[:, i * n : (i + 1) * n],
                    in_=table[:].indirect(offsets[:, i * n // 16 : (i + 1) * n // 16]),
                )
            return picked

        w1_codes = {}
        w1_plane = {}

        def round_w1(b, a, copy, slot=None):
            name = "w1_bf16_%d_%d" % (b, a)
            shape = [P, PACK * PASS]
            grouped = held(shape, BF16, name) if slot is None else streamed(slot, shape, BF16, name)
            for u in range(2):
                copy(
                    out=grouped[:, u * 2 * PASS : (u + 1) * 2 * PASS].rearrange("p (e m j) -> p m j e", e=2, j=PACK),
                    in_=w1_raw[(b, a)][:].rearrange("p j (m u e) -> p u m j e", u=2, e=2)[:, u],
                )
            return grouped

        def quantise_w1(b, a, grouped, slot=None):
            name = "w1_codes_%d_%d" % (b, a)
            codes = held([P, PASS], U32, name) if slot is None else streamed(slot, [P, PASS], U32, name)
            plane = held([P, PASS], U8, "w1_plane_%d_%d" % (b, a))
            for u in range(2):
                cols = slice(u * 2 * P, (u + 1) * 2 * P)
                nc.vector.quantize_mx(
                    out=codes[:, cols].bitcast(FP8X4),
                    scales=plane[:, cols],
                    in_=grouped[:, u * 2 * PASS : (u + 1) * 2 * PASS],
                )
            w1_codes[(b, a)] = codes
            w1_plane[(b, a)] = plane

        def banks(group, name):
            return [psum.tile([P, PASS], F32, name="%s%d" % (name, i), tag="%s%d" % (group, i)) for i in range(4)]

        v_codes = []

        def h2_pass(bank, b, a):
            for jh in range(2):
                cols = slice(jh * HALF, (jh + 1) * HALF)
                for u in range(2):
                    for e in range(2):
                        first = b * PASS + (2 * u + e) * P
                        nc.tensor.matmul_mx(
                            out=bank[2 * jh + u][:, e * HALF : (e + 1) * HALF],
                            lhsT=w4_codes[:, a, first : first + P].bitcast(FP4X4),
                            lhsT_scale=k_plane[a][:, S + first : S + first + P],
                            rhs=v_codes[a][:, cols].bitcast(FP8X4),
                            rhs_scale=k_plane[a][:, cols],
                            start=(a == 0 and e == 0),
                            stop=(a == K_PASSES - 1 and e == 1),
                        )

        def h2_out(bank, b, slot):
            halves = []
            for jh in range(2):
                h2 = streamed(slot + jh, [P, 2, HALF, 2], F32, "h2_%d_%d" % (b, jh))
                for u in range(2):
                    nc.scalar.copy(out=h2[:, u, :, :], in_=bank[2 * jh + u][:].rearrange("p (e j) -> p j e", e=2))
                halves.append(h2)
            return halves

        def h1_pass(bank, b, a):
            for c in range(CHUNKS):
                cols = slice(c * CHUNK, (c + 1) * CHUNK)
                for t in range(PACK):
                    nc.tensor.matmul_mx(
                        out=bank[c][:, t * CHUNK : (t + 1) * CHUNK],
                        lhsT=w1_codes[(b, a)][:, t * P : (t + 1) * P].bitcast(FP8X4),
                        lhsT_scale=w1_plane[(b, a)][:, t * P : (t + 1) * P],
                        rhs=v_codes[a][:, cols].bitcast(FP8X4),
                        rhs_scale=k_plane[a][:, cols],
                        start=(a == 0 and t == 0),
                        stop=(a == K_PASSES - 1 and t == PACK - 1),
                    )

        def extreme(dst, bank, h2, c, op):
            j0 = (c % 2) * CHUNK
            nc.vector.tensor_tensor(
                out=dst[:, c * PASS : (c + 1) * PASS].rearrange("p (j u e) -> p j u e", u=2, e=2),
                in0=bank[c][:].rearrange("p (u e j) -> p j u e", u=2, e=2),
                in1=h2[c // 2][:, :, j0 : j0 + CHUNK, :].rearrange("p u j e -> p j u e"),
                op=op,
            )

        def quantise_h(src, name):
            codes = held([P, S], U32, name + "_codes")
            plane = held([P, S], U8, name + "_plane")
            nc.vector.quantize_mx(out=codes[:].bitcast(FP8X4), scales=plane[:], in_=src[:])
            return codes, plane

        def e_pass(bank, picked, first, h, b):
            for mt in range(4):
                nc.tensor.matmul_mx(
                    out=bank[mt][:],
                    lhsT=picked[:, mt * P : (mt + 1) * P].bitcast(FP8X4),
                    lhsT_scale=r_planes[R_PLANE:P, b, first + mt * P : first + (mt + 1) * P],
                    rhs=h[0][:].bitcast(FP8X4),
                    rhs_scale=h[1][:],
                    start=(b == 0),
                    stop=(b == R_BLOCKS - 1),
                )

        h2_bank = [banks("low", "h2_first"), banks("high", "h2_second")]
        v_codes.append(gather_words(v_table[0], list1, "v_codes0"))
        for b in range(R_BLOCKS):
            h2_pass(h2_bank[b], b, 0)
        r_picked_rows = streamed(2, [P, 2 * S], U8, "r_picked_rows")
        nc.vector.tensor_copy(out=r_picked_rows[:, 0:S], in_=v2_rows[:].indirect(list2[:]))
        v_table.append(load_words(3, tab_words, 2, "v_table2"))
        v_codes.append(gather_words(v_table[1], list1, "v_codes1"))
        w1_raw[(0, 1)] = load_w1(0, 0, 1)
        for b in range(R_BLOCKS):
            h2_pass(h2_bank[b], b, 1)
        nc.vector.tensor_copy(out=r_picked_rows[:, S:], in_=v3_rows[:].indirect(list3[:]))
        w1_raw[(0, 2)] = load_w1(4, 0, 2)
        per_quad = PACK * R_BLOCKS
        for q in QUAD_ORDER:
            nc.gpsimd.dma_start(
                out=r_planes[32 * q + R_PLANE : 32 * q + R_PLANE + PACK, :, :].bitcast(I32),
                in_=r_picked_rows[per_quad * q : per_quad * (q + 1), :].bitcast(I32),
            )
        v_codes.append(gather_words(v_table[2], list1, "v_codes2"))
        quantise_w1(0, 0, round_w1(0, 0, nc.scalar.copy))
        w1_raw[(1, 0)] = load_w1(1, 1, 0)
        w1_raw[(1, 1)] = load_w1(3, 1, 1)
        for b in range(R_BLOCKS):
            h2_pass(h2_bank[b], b, 2)
        h2_first = h2_out(h2_bank[0], 0, 6)
        h2_second = h2_out(h2_bank[1], 1, 8)
        h1_bank = banks("low", "h1_first")
        h1_pass(h1_bank, 0, 0)
        quantise_w1(0, 1, round_w1(0, 1, nc.vector.tensor_copy))
        w1_raw[(1, 2)] = load_w1(0, 1, 2)
        h1_pass(h1_bank, 0, 1)
        quantise_w1(0, 2, round_w1(0, 2, nc.vector.tensor_copy, slot=5))
        v2_table = [load_words(4, tab2_words, 0, "v2_table0"), load_words(5, tab2_words, 1, "v2_table1")]
        h1_pass(h1_bank, 0, 2)
        rounded = [round_w1(1, 0, nc.scalar.copy)]
        v3_table = [load_words(1, tab3_words, 0, "v3_table0")]

        hi_first = held([P, PACK * S], BF16, "hi_first")
        lo_first = held([P, PACK * S], BF16, "lo_first")
        for c in range(CHUNKS):
            extreme(hi_first, h1_bank, h2_first, c, ALU.max)
            extreme(lo_first, h1_bank, h2_first, c, ALU.min)
        rounded.append(round_w1(1, 1, nc.scalar.copy))
        v3_table.append(load_words(3, tab3_words, 1, "v3_table1"))
        quantise_w1(1, 0, rounded[0], slot=6)
        quantise_w1(1, 1, rounded[1], slot=7)
        hi = [quantise_h(hi_first, "hi0")]
        lo = [quantise_h(lo_first, "lo0")]
        rounded.append(round_w1(1, 2, nc.scalar.copy))
        sums = streamed(0, [P, 4, S], F32, "sums")
        for i in range(2):
            rows = prior[2 * i * P : 2 * (i + 1) * P, :]
            nc.sync.dma_start(out=sums[:, 2 * i : 2 * i + 2, :], in_=rows.rearrange("(m p) j -> p m j", p=P))
        result = [sums[:, mt, :] for mt in range(4)]
        h1_bank = banks("high", "h1_second")
        for a in range(K_PASSES - 1):
            h1_pass(h1_bank, 1, a)
        v2_first = gather_words(v2_table[0], list2, "v2_codes0")
        quantise_w1(1, 2, rounded[2])
        h1_pass(h1_bank, 1, 2)

        e2_bank = banks("low", "e2")
        e_pass(e2_bank, v2_first, 0, hi[0], 0)
        hi_second = held([P, PACK * S], BF16, "hi_second")
        lo_second = held([P, PACK * S], BF16, "lo_second")
        for c in range(CHUNKS):
            extreme(hi_second, h1_bank, h2_second, c, ALU.max)
        extreme(lo_second, h1_bank, h2_second, 0, ALU.min)
        hi.append(quantise_h(hi_second, "hi1"))
        e_pass(e2_bank, gather_words(v2_table[1], list2, "v2_codes1"), 0, hi[1], 1)
        for c in range(1, CHUNKS):
            extreme(lo_second, h1_bank, h2_second, c, ALU.min)
        gate = []
        for mt in range(4):
            tile = held([P, S], F32, "gate%d" % mt)
            nc.scalar.activation(out=tile[:], in_=e2_bank[mt][:], func=ACT.Tanh)
            gate.append(tile)
        e3_bank = banks("high", "e3")
        e_pass(e3_bank, gather_words(v3_table[0], list3, "v3_codes0"), S, lo[0], 0)
        lo.append(quantise_h(lo_second, "lo1"))
        e_pass(e3_bank, gather_words(v3_table[1], list3, "v3_codes1", pieces=2), S, lo[1], 1)

        for mt in range(4):
            nc.vector.tensor_tensor(out=gate[mt][:], in0=e3_bank[mt][:], in1=gate[mt][:], op=ALU.mult)
            if mt > 0:
                adder = nc.gpsimd if mt == 1 else nc.vector
                adder.tensor_tensor(out=result[mt - 1], in0=result[mt - 1], in1=gate[mt - 1][:], op=ALU.add)
                nc.sync.dma_start(out=out[(mt - 1) * P : mt * P, :], in_=result[mt - 1])
        nc.vector.tensor_tensor(out=result[3], in0=result[3], in1=gate[3][:], op=ALU.add)
        nc.sync.dma_start(out=out[3 * P : 4 * P, :], in_=result[3])
